import numpy as np, ml_dtypes
CORES = [10,34,74,98]
N = 4
import mx_ref
NC, G, GR = 128, 4, 2
C = np.float32(0.023)
BF = ml_dtypes.bfloat16
def cut(t, i, w=512):
    return t[:, w * i:w * i + w]
def tile(rs):
    return np.stack(rs, axis=2).reshape(128, -1).astype(BF)
def layer(w, X):
    out = []
    for i in range(G):
        for t in range(len(X)):
            p = mx_ref.matmul(mx_ref.quantize(cut(w, len(X) * i + t)), X[t])
            z = p if t == 0 else z + p
        out.append(z)
    return out
def act(Z):
    return [np.maximum(z, 0) * C for z in Z]
def setup_inputs(rng):
    def f(*shape):
        return mx_ref.flush((rng.standard_normal(shape, dtype=np.float32) * np.exp2(rng.integers(-2, 3, shape[:-1] + (1,)))).astype(BF))
    return {"xa": f(N, 128, 512), "xb": f(N, 128, 4 * NC), "wa": f(N, 128, G * 512), "wb": f(N, 128, G * 512)}
def setup_inputs_blocks(rng):
    d = setup_inputs(rng)
    for k in ("xa", "xb", "wa", "wb"): d[k] = mx_ref.spread(d[k], rng, 2)
    return d
def setup_inputs_wide(rng):
    d = setup_inputs(rng)
    for k in ("xa", "xb", "wa", "wb"): d[k] = mx_ref.flush((d[k].astype(np.float32) * np.exp2(rng.integers(-5, 6, (N, 1, 1))).astype(np.float32)).astype(BF))
    return d
def reference(xa, xb, wa, wb):
    A = [mx_ref.quantize(tile(act(layer(wa[j], [mx_ref.quantize(xa[j])])))) for j in range(N)]
    M = [mx_ref.quantize(tile(act(layer(wb[j], [mx_ref.quantize(xb[j])])))) for j in range(N)]
    y = np.zeros((N, 128, NC), np.float32)
    for r in range(N):
        i, j = divmod(r, GR)
        for k in range(GR):
            p = mx_ref.matmul(A[GR * i + k], M[GR * k + j])
            y[r] = p if k == 0 else y[r] + p
    return {"y": y}

import numpy as np
from concourse.mybir import dt, AluOpType, ActivationFunctionType

NC, G, GR, W = 128, 4, 2, 512
C = float(np.float32(0.023))

SCRATCH = {"yout": ("sbuf", [128, NC], "float32")}
SEMAPHORES = ["sent", "mmy", "copied", "stored"]
for _m in "ab":
    SCRATCH["x" + _m + "_in"] = ("sbuf", [128, W], "bfloat16")
    SCRATCH["w" + _m + "_in"] = ("sbuf", [128, G * W], "bfloat16")
    SCRATCH["xq_" + _m] = ("sbuf", [128, NC], "float8_e4m3fn_x4")
    SCRATCH["xs_" + _m] = ("sbuf", [128, NC], "uint8")
    SCRATCH["wq_" + _m] = ("sbuf", [128, G * NC], "float8_e4m3fn_x4")
    SCRATCH["ws_" + _m] = ("sbuf", [128, G * NC], "uint8")
    SCRATCH["tile_" + _m] = ("sbuf", [128, G * NC], "bfloat16")
    SCRATCH["own_q_" + _m] = ("sbuf", [128, NC], "float8_e4m3fn_x4")
    SCRATCH["own_s_" + _m] = ("sbuf", [128, NC], "uint8")
    SCRATCH["far_q_" + _m] = ("sbuf", [128, NC], "float8_e4m3fn_x4")
    SCRATCH["far_s_" + _m] = ("sbuf", [128, NC], "uint8")
    SCRATCH["z_" + _m] = ("psum", [128, G * 512], "float32")
    SEMAPHORES += [s + "_" + _m for s in ("ldx", "ldw", "ldl", "qx", "act", "qt", "arr")]
    SEMAPHORES += ["%s%d_%s" % (s, i, _m) for s in ("qw", "mm") for i in range(G)]


def rank_program(g, core, T, topo):
    rank = T.rank_of(core)
    if rank is None:
        return
    row, col = divmod(rank, GR)
    peer = {"a": T.cores[GR * row + (1 - col)], "b": T.cores[GR * (1 - row) + col]}
    straight = {m: topo.same_plane(topo.chip(core), topo.chip(peer[m])) for m in "ab"}
    order = "ba" if straight["a"] and not straight["b"] else "ab"
    sem = T.sem
    last = G - 1

    for m in order:
        g.sync.dma_start(T["x" + m + "_in"][:], T["x" + m][:]).then_inc(sem["ldx_" + m], 16)
        g.sync.dma_start(T["w" + m + "_in"][:, 0:last * W], T["w" + m][:, 0:last * W]).then_inc(sem["ldw_" + m], 16)
        g.sync.dma_start(T["w" + m + "_in"][:, last * W:G * W], T["w" + m][:, last * W:G * W]).then_inc(sem["ldl_" + m], 16)

    for m in order:
        xq, xs, wq, ws = T["xq_" + m], T["xs_" + m], T["wq_" + m], T["ws_" + m]
        z, t = T["z_" + m], T["tile_" + m]
        g.vector.wait_ge(sem["ldx_" + m], 16)
        g.vector.quantize_mx(xq[:], xs[:], T["x" + m + "_in"][:]).then_inc(sem["qx_" + m], 1)
        g.tensor.wait_ge(sem["qx_" + m], 1)
        for i in range(G):
            if i == 0:
                g.vector.wait_ge(sem["ldw_" + m], 16)
            if i == last:
                g.vector.wait_ge(sem["ldl_" + m], 16)
            c0, c1 = i * NC, (i + 1) * NC
            g.vector.quantize_mx(wq[:, c0:c1], ws[:, c0:c1], T["w" + m + "_in"][:, i * W:(i + 1) * W]).then_inc(sem["qw%d_%s" % (i, m)], 1)
            g.tensor.wait_ge(sem["qw%d_%s" % (i, m)], 1)
            g.tensor.matmul_mx(z[:, 512 * i:512 * i + NC], wq[:, c0:c1], ws[:, c0:c1], xq[:], xs[:], True, True).then_inc(sem["mm%d_%s" % (i, m)], 1)
            if i < last:
                g.scalar.wait_ge(sem["mm%d_%s" % (i, m)], 1)
                g.scalar.activation(t[:, i:G * NC:G], z[:, 512 * i:512 * i + NC], ActivationFunctionType.Relu, scale=C).then_inc(sem["act_" + m], 1)
            else:
                g.vector.wait_ge(sem["mm%d_%s" % (i, m)], 1)
                g.vector.tensor_scalar(t[:, i:G * NC:G], z[:, 512 * i:512 * i + NC], 0.0, C, AluOpType.max, AluOpType.mult).then_inc(sem["act_" + m], 1)
        g.vector.wait_ge(sem["act_" + m], G)
        g.vector.quantize_mx(T["own_q_" + m][:], T["own_s_" + m][:], t[:]).then_inc(sem["qt_" + m], 1)

        dst = peer[m]
        rid, pid, _ = topo.addr(dst)
        mask = topo.mask(core, dst)
        g.wait_ge(sem["qt_" + m], 1)
        g.remote_dma(T["far_q_" + m][:].bitcast(dt.uint8), T["own_q_" + m][:].bitcast(dt.uint8), sem["arr_" + m], sem["sent"], pid, rid, mask)
        g.remote_dma(T["far_s_" + m][:], T["own_s_" + m][:], sem["arr_" + m], sem["sent"], pid, rid, mask)

    engines = {m: bin(topo.mask(core, peer[m])).count("1") for m in "ab"}
    landed = {m: 2 * bin(topo.mask(peer[m], core)).count("1") for m in "ab"}

    m1, m2 = order
    slices = []
    for k in range(GR):
        slices.append({"a": k == col, "b": k == row})
    slices.sort(key=lambda s: (not s[m2], not s[m1]))
    yz = T["z_" + m1][:, 0:NC]
    waited = []
    for n, s in enumerate(slices):
        src = {}
        for m in (m1, m2):
            src[m] = "own" if s[m] else "far"
            if (m, src[m]) not in waited:
                waited.append((m, src[m]))
                if s[m]:
                    g.tensor.wait_ge(sem["qt_" + m], 1)
                else:
                    g.tensor.wait_ge(sem["arr_" + m], landed[m])
        op = g.tensor.matmul_mx(yz, T[src["a"] + "_q_a"][:], T[src["a"] + "_s_a"][:], T[src["b"] + "_q_b"][:], T[src["b"] + "_s_b"][:], n == 0, n == GR - 1)
        if n == GR - 1:
            op.then_inc(sem["mmy"], 1)

    g.vector.wait_ge(sem["mmy"], 1)
    g.vector.tensor_copy(T.yout[:], yz).then_inc(sem["copied"], 1)
    g.sync.wait_ge(sem["copied"], 1)
    g.sync.dma_start(T.y[:], T.yout[:]).then_inc(sem["stored"], 16)
    g.sync.wait_ge(sem["stored"], 16)
    g.wait_ge(sem["sent"], 2 * (engines["a"] + engines["b"]))
